import numpy as np
import ml_dtypes


def mxq(x, axis, fmt="e4m3"):
    dtype, down = {"e4m3": (ml_dtypes.float8_e4m3fn, 7), "e5m2": (ml_dtypes.float8_e5m2, 14)}[fmt]
    v = np.moveaxis(np.asarray(x, np.float32).astype(ml_dtypes.bfloat16).astype(np.float64), axis, -1)
    blocks = v.reshape(v.shape[:-1] + (-1, 32))
    amax = np.abs(blocks).max(-1, keepdims=True)
    byte = np.maximum(np.where(amax > 0, np.frexp(amax)[1] - 1 + 127, 0) - down, 1)
    scale = np.exp2(byte - 127.0)
    codes = (blocks / scale).astype(np.float32).astype(dtype).astype(np.float64)
    return np.moveaxis((codes * scale).reshape(v.shape), -1, axis)


WIDE = False


def mx_kscale(k, group=512):
    if not WIDE:
        return np.ones(k)
    levels = np.array([10, -10, 5, -5, 0])
    if group != 512:
        return np.exp2(np.random.permutation(np.resize(levels, k // group))).repeat(group)
    if k % 512:
        return np.exp2(np.random.permutation(np.resize(levels, k // 32))).repeat(32)
    a = np.empty((k // 512, 16))
    for p in range(k // 512):
        a[p, :8] = np.random.permutation(np.resize(levels, 8))
        for g in range(8):
            far = levels[np.abs(levels - a[p, g]) >= 10]
            a[p, g + 8] = far[np.random.randint(len(far))]
    return np.exp2(a.ravel()).repeat(32)


def f64(x):
    return np.asarray(x).astype(np.float64)


E2M1 = np.array([0.0, 0.5, 1.0, 1.5, 2.0, 3.0, 4.0, 6.0, -0.0, -0.5, -1.0, -1.5, -2.0, -3.0, -4.0, -6.0])


def pack_group(w):
    k, n = w.shape
    w = f64(np.asarray(w, np.float32).astype(ml_dtypes.bfloat16)).reshape(k // 32, 32, n)
    amax = np.abs(w).max(1)
    mant, ex = np.frexp(amax / 6.0)
    byte = np.clip(np.where(amax > 0, np.where(mant > 0.5, ex, ex - 1) + 127, 1), 1, 254)
    scaled = (w * np.exp2(127.0 - byte)[:, None, :]).reshape(k, n).astype(np.float32)
    c = np.ascontiguousarray(scaled.reshape(k // 4, 4, n).transpose(0, 2, 1)).astype(ml_dtypes.float4_e2m1fn).view(np.uint8) & 0xF
    return np.ascontiguousarray((c[..., 0::2] | (c[..., 1::2] << 4)).reshape(k // 4, 2 * n)), byte.astype(np.uint8)


def unpack_group(words, scales):
    p, n = words.shape[0], scales.shape[1]
    words = np.ascontiguousarray(words).reshape(p, n, 2)
    nib = np.empty((p, n, 4), np.uint8)
    nib[..., 0::2] = words & 0xF
    nib[..., 1::2] = words >> 4
    return E2M1[nib].transpose(0, 2, 1).reshape(4 * p, n) * np.repeat(np.exp2(scales.astype(np.float64) - 127.0), 32, axis=0)


def sigmoid(v):
    return 1.0 / (1.0 + np.exp(-v))


G, D, M, O, N = 2, 256, 256, 256, 512


def setup_inputs():
    n = np.random.standard_normal
    s_d = mx_kscale(D, 0)
    s_o = mx_kscale(O, 0)
    w1_ = [pack_group(w) for w in n((G, D, M)) / np.sqrt(D) / s_d[:, None]]
    w2_ = [pack_group(w) for w in n((G, D, M)) / np.sqrt(D) / s_d[:, None]]
    w3_ = [pack_group(w) for w in n((G, D, M)) / np.sqrt(D) / s_d[:, None]]
    wo_ = [pack_group(w) for w in n((G, O, M)) / np.sqrt(O) / s_o[:, None]]
    return {
        "x": (n((G, D, N)) * s_d[:, None]).astype(np.float32),
        "w1_words": np.stack([w[0] for w in w1_]),
        "w1_scales": np.stack([w[1] for w in w1_]),
        "w2_words": np.stack([w[0] for w in w2_]),
        "w2_scales": np.stack([w[1] for w in w2_]),
        "w3_words": np.stack([w[0] for w in w3_]),
        "w3_scales": np.stack([w[1] for w in w3_]),
        "wo_words": np.stack([w[0] for w in wo_]),
        "wo_scales": np.stack([w[1] for w in wo_]),
        "dy": (n((G, O, N)) * s_o[:, None]).astype(np.float32),
        "old": (0.3 * n((G, M, N))).astype(np.float32),
    }


def reference(x, w1_words, w1_scales, w2_words, w2_scales, w3_words, w3_scales, wo_words, wo_scales, dy, old):
    w1 = np.stack([unpack_group(w1_words[g], w1_scales[g]) for g in range(G)])
    xq = mxq(f64(x), 1, "e4m3")
    z1 = w1.transpose(0, 2, 1) @ xq
    w2 = np.stack([unpack_group(w2_words[g], w2_scales[g]) for g in range(G)])
    z2 = w2.transpose(0, 2, 1) @ xq
    w3 = np.stack([unpack_group(w3_words[g], w3_scales[g]) for g in range(G)])
    z3 = w3.transpose(0, 2, 1) @ xq
    sg = sigmoid(z1 * z2 + z3)
    wo = np.stack([unpack_group(wo_words[g], wo_scales[g]) for g in range(G)])
    dyq = mxq(f64(dy), 1, "e4m3")
    c0 = wo.transpose(0, 2, 1) @ dyq
    dsg = c0 * np.tanh(z3)
    dz3 = c0 * sg * (1.0 - np.square(np.tanh(z3))) + dsg * sg * (1.0 - sg)
    y = dz3 + f64(old)
    return y

@@ -1,0 +1,214 @@
+from contextlib import ExitStack
+
+import concourse.mybir as mybir
+
+G, D, M, N = 2, 256, 256, 512
+FLOPS = 2 * 4 * G * D * M * N
+
+F32 = mybir.dt.float32
+BF16 = mybir.dt.bfloat16
+I32 = mybir.dt.int32
+U32 = mybir.dt.uint32
+U8 = mybir.dt.uint8
+FP8X4 = mybir.dt.float8_e4m3fn_x4
+FP4X4 = mybir.dt.float4_e2m1fn_x4
+ACT = mybir.ActivationFunctionType
+ALU = mybir.AluOpType
+
+P = 128
+PACK = 4
+ROWS = 64
+VECTOR_COLS = 336
+
+
+def tile_rows_bbilinsig_kernel(
+    tc, x, w1_words, w1_scales, w2_words, w2_scales, w3_words, w3_scales, wo_words, wo_scales, dy, old, out
+):
+    nc = tc.nc
+    with ExitStack() as ctx:
+        sb = ctx.enter_context(tc.tile_pool(name="sb", bufs=1))
+        ps = ctx.enter_context(tc.psum_pool(name="ps", bufs=1))
+        ctx.enter_context(tc.manual_schedule())
+
+        w_dram = [w1_words, w2_words, w3_words, wo_words]
+        s_dram = [w1_scales, w2_scales, w3_scales, wo_scales]
+        words = [sb.tile([P, 2 * M], U8, name="words%d" % w, align_bytes=64) for w in range(4)]
+        plane = sb.tile([P, 4 * M], U8, name="plane", align_bytes=64)
+        x_raw = sb.tile([P, PACK, N], F32, name="x_raw")
+        dy_raw = sb.tile([P, PACK, N], F32, name="dy_raw")
+        old_sb = sb.tile([P, 4, N], F32, name="old_sb")
+        x_bf = sb.tile([P, N, PACK], BF16, name="x_bf", align_bytes=64)
+        dy_bf = sb.tile([P, N, PACK], BF16, name="dy_bf", align_bytes=64)
+        x_codes = sb.tile([P, N], U32, name="x_codes", align_bytes=64)
+        dy_codes = sb.tile([P, N], U32, name="dy_codes", align_bytes=64)
+        x_scales = sb.tile([P, N], U8, name="x_scales", align_bytes=64)
+        dy_scales = sb.tile([P, N], U8, name="dy_scales", align_bytes=64)
+        zero = sb.tile([P, 1], F32, name="zero")
+        half = sb.tile([P, 1], F32, name="half")
+        bank = [[ps.tile([P, N], F32, name="bank%d_%d" % (w, g)) for g in range(G)] for w in range(4)]
+
+        def stage(name):
+            return [sb.tile([P, N], F32, name="%s%d" % (name, i)) for i in range(4)]
+
+        z1c, prod, u, th, sg, sq, ts, n_, gc, neg, res = [
+            stage(nm) for nm in ("z1c", "prod", "u", "th", "sg", "sq", "ts", "n", "gc", "neg", "res")
+        ]
+
+        def load_words(w):
+            nc.sync.dma_start(
+                out=words[w][:].bitcast(I32), in_=w_dram[w].rearrange("g p b -> (g p) b").bitcast(I32)
+            )
+
+        def load_scales(engine, w, quads):
+            rows = s_dram[w].rearrange("g (c r) m -> (g c) r m", r=4)
+            for q in quads:
+                engine.dma_start(
+                    out=plane[32 * q : 32 * q + 4, M * w : M * (w + 1)].bitcast(I32), in_=rows[q].bitcast(I32)
+                )
+
+        def load_packed(raw, src):
+            nc.sync.dma_start(out=raw[:], in_=src.rearrange("g (p j) n -> (g p) j n", j=PACK))
+
+        def views(raw, bf, c0, c1):
+            dst = bf[:, c0:c1, :].rearrange("p (c i) j -> p c j i", i=4)
+            src = raw[:, :, c0:c1].rearrange("p j (c i) -> p c j i", i=4)
+            return dst, src
+
+        def quantize(bf, codes, scales):
+            nc.vector.quantize_mx(
+                out=codes[:].bitcast(FP8X4), scales=scales[:], in_=bf[:].rearrange("p n j -> p (n j)")
+            )
+
+        def product(w, i):
+            h, g = divmod(i, G)
+            rows = slice(ROWS * g, ROWS * (g + 1))
+            codes, scales = (dy_codes, dy_scales) if w == 3 else (x_codes, x_scales)
+            nc.tensor.matmul_mx(
+                out=bank[w][g][:],
+                lhsT=words[w][rows, 2 * P * h : 2 * P * (h + 1)].bitcast(FP4X4),
+                lhsT_scale=plane[rows, M * w + P * h : M * w + P * (h + 1)],
+                rhs=codes[rows, :].bitcast(FP8X4),
+                rhs_scale=scales[rows, :],
+                start=True,
+                stop=True,
+            )
+
+        def copy_z1(i):
+            nc.scalar.copy(out=z1c[i][:], in_=bank[0][i % G][:])
+
+        def mul_z2(i):
+            nc.vector.tensor_tensor(out=prod[i][:], in0=z1c[i][:], in1=bank[1][i % G][:], op=ALU.mult)
+
+        def add_z3(i):
+            nc.vector.tensor_tensor(out=u[i][:], in0=prod[i][:], in1=bank[2][i % G][:], op=ALU.add)
+
+        def tanh_z3(i):
+            nc.scalar.activation(out=th[i][:], in_=bank[2][i % G][:], func=ACT.Tanh)
+
+        def sigmoid_u(i):
+            nc.scalar.activation(out=sg[i][:], in_=u[i][:], func=ACT.Sigmoid)
+
+        def square_t(i):
+            nc.scalar.activation(out=sq[i][:], in_=th[i][:], func=ACT.Square, bias=half[:], scale=-1.0)
+
+        def mul_ts(i):
+            nc.vector.tensor_tensor(out=ts[i][:], in0=th[i][:], in1=sg[i][:], op=ALU.mult)
+
+        def add_sq(engine, i):
+            engine.tensor_tensor(out=n_[i][:], in0=ts[i][:], in1=sq[i][:], op=ALU.add)
+
+        def mul_c0(i):
+            nc.vector.scalar_tensor_tensor(
+                out=gc[i][:], in0=n_[i][:], scalar=1.25, in1=bank[3][i % G][:], op0=ALU.subtract, op1=ALU.mult
+            )
+
+        def mul_sg(i):
+            nc.vector.tensor_tensor(out=neg[i][:], in0=gc[i][:], in1=sg[i][:], op=ALU.mult)
+
+        def finish(engine, i):
+            h, g = divmod(i, G)
+            engine.tensor_tensor(out=res[i][:], in0=old_sb[:, 2 * g + h, :], in1=neg[i][:], op=ALU.subtract)
+            nc.sync.dma_start(out=out[g, P * h : P * (h + 1), :], in_=res[i][:])
+
+        nc.vector.memset(plane[:].bitcast(I32), 0)
+        nc.gpsimd.memset(zero[:], 0.0)
+        nc.scalar.activation(out=half[:], in_=zero[:], func=ACT.Sigmoid)
+
+        load_words(0)
+        load_packed(x_raw, x)
+        load_words(1)
+        load_scales(nc.sync, 0, range(4))
+        load_words(2)
+        load_scales(nc.gpsimd, 1, range(4))
+        load_packed(dy_raw, dy)
+        load_scales(nc.sync, 2, range(4))
+        load_words(3)
+        load_scales(nc.sync, 3, range(4))
+        nc.sync.dma_start(out=old_sb[:], in_=old.rearrange("g (h p) n -> p (g h) n", p=P))
+
+        dst, src = views(x_raw, x_bf, 0, VECTOR_COLS)
+        nc.vector.tensor_copy(out=dst, in_=src)
+        dst, src = views(x_raw, x_bf, VECTOR_COLS, N)
+        nc.scalar.copy(out=dst, in_=src)
+        quantize(x_bf, x_codes, x_scales)
+        for w in range(3):
+            product(w, 0)
+            product(w, 1)
+
+        dst, src = views(dy_raw, dy_bf, 0, N)
+        nc.gpsimd.tensor_scalar(out=dst, in0=src, scalar1=1.0, scalar2=0.0, op0=ALU.mult, op1=ALU.add)
+
+        copy_z1(0)
+        copy_z1(1)
+        mul_z2(0)
+        mul_z2(1)
+        for w in range(2):
+            product(w, 2)
+            product(w, 3)
+        tanh_z3(0)
+        tanh_z3(1)
+        add_z3(0)
+        add_z3(1)
+        product(2, 2)
+        product(2, 3)
+        sigmoid_u(0)
+        sigmoid_u(1)
+        quantize(dy_bf, dy_codes, dy_scales)
+        product(3, 0)
+        product(3, 1)
+        square_t(0)
+        square_t(1)
+        mul_ts(0)
+        mul_ts(1)
+        add_sq(nc.vector, 0)
+        add_sq(nc.gpsimd, 1)
+        copy_z1(2)
+        tanh_z3(2)
+        copy_z1(3)
+        square_t(2)
+        mul_z2(2)
+        mul_c0(0)
+        product(3, 2)
+        add_z3(2)
+        sigmoid_u(2)
+        mul_sg(0)
+        finish(nc.gpsimd, 0)
+        tanh_z3(3)
+        square_t(3)
+        mul_z2(3)
+        mul_c0(1)
+        product(3, 3)
+        add_z3(3)
+        sigmoid_u(3)
+        mul_ts(2)
+        mul_ts(3)
+        add_sq(nc.vector, 2)
+        mul_sg(1)
+        add_sq(nc.vector, 3)
+        finish(nc.gpsimd, 1)
+        mul_c0(2)
+        mul_c0(3)
+        mul_sg(2)
+        mul_sg(3)
+        finish(nc.vector, 2)
+        finish(nc.vector, 3)

@@ -18,7 +18,7 @@ ALU = mybir.AluOpType
 P = 128
 PACK = 4
 ROWS = 64
-VECTOR_COLS = 336
+VECTOR_COLS = 320
 
 
 def tile_rows_bbilinsig_kernel(
@@ -35,7 +35,7 @@ def tile_rows_bbilinsig_kernel(
         words = [sb.tile([P, 2 * M], U8, name="words%d" % w, align_bytes=64) for w in range(4)]
         plane = sb.tile([P, 4 * M], U8, name="plane", align_bytes=64)
         x_raw = sb.tile([P, PACK, N], F32, name="x_raw")
-        dy_raw = sb.tile([P, PACK, N], F32, name="dy_raw")
+        dy_raw = [sb.tile([P, PACK, N // 2], F32, name="dy_raw%d" % k) for k in range(2)]
         old_sb = sb.tile([P, 4, N], F32, name="old_sb")
         x_bf = sb.tile([P, N, PACK], BF16, name="x_bf", align_bytes=64)
         dy_bf = sb.tile([P, N, PACK], BF16, name="dy_bf", align_bytes=64)
@@ -66,17 +66,17 @@ def tile_rows_bbilinsig_kernel(
                     out=plane[32 * q : 32 * q + 4, M * w : M * (w + 1)].bitcast(I32), in_=rows[q].bitcast(I32)
                 )
 
-        def load_packed(raw, src):
-            nc.sync.dma_start(out=raw[:], in_=src.rearrange("g (p j) n -> (g p) j n", j=PACK))
+        def load_packed(raw, src, c0, c1):
+            nc.sync.dma_start(out=raw[:], in_=src.rearrange("g (p j) n -> (g p) j n", j=PACK)[:, :, c0:c1])
 
-        def views(raw, bf, c0, c1):
-            dst = bf[:, c0:c1, :].rearrange("p (c i) j -> p c j i", i=4)
-            src = raw[:, :, c0:c1].rearrange("p j (c i) -> p c j i", i=4)
-            return dst, src
+        def views(raw, bf):
+            return bf.rearrange("p (c i) j -> p c j i", i=4), raw.rearrange("p j (c i) -> p c j i", i=4)
 
-        def quantize(bf, codes, scales):
+        def quantize(bf, codes, scales, c0, c1):
             nc.vector.quantize_mx(
-                out=codes[:].bitcast(FP8X4), scales=scales[:], in_=bf[:].rearrange("p n j -> p (n j)")
+                out=codes[:, c0:c1].bitcast(FP8X4),
+                scales=scales[:, c0:c1],
+                in_=bf[:, c0:c1, :].rearrange("p n j -> p (n j)"),
             )
 
         def product(w, i):
@@ -125,38 +125,47 @@ def tile_rows_bbilinsig_kernel(
         def mul_sg(i):
             nc.vector.tensor_tensor(out=neg[i][:], in0=gc[i][:], in1=sg[i][:], op=ALU.mult)
 
-        def finish(engine, i):
+        def finish(engine, i, c0=0, c1=N):
             h, g = divmod(i, G)
-            engine.tensor_tensor(out=res[i][:], in0=old_sb[:, 2 * g + h, :], in1=neg[i][:], op=ALU.subtract)
-            nc.sync.dma_start(out=out[g, P * h : P * (h + 1), :], in_=res[i][:])
+            engine.tensor_tensor(
+                out=res[i][:, c0:c1], in0=old_sb[:, 2 * g + h, c0:c1], in1=neg[i][:, c0:c1], op=ALU.subtract
+            )
+            nc.sync.dma_start(out=out[g, P * h : P * (h + 1), c0:c1], in_=res[i][:, c0:c1])
 
         nc.vector.memset(plane[:].bitcast(I32), 0)
         nc.gpsimd.memset(zero[:], 0.0)
         nc.scalar.activation(out=half[:], in_=zero[:], func=ACT.Sigmoid)
 
         load_words(0)
-        load_packed(x_raw, x)
+        load_packed(x_raw, x, 0, N)
         load_words(1)
-        load_scales(nc.sync, 0, range(4))
+        load_scales(nc.sync, 0, range(2))
+        load_scales(nc.sync, 1, range(2))
+        load_scales(nc.sync, 0, range(2, 3))
+        load_scales(nc.gpsimd, 2, range(2, 4))
+        load_packed(dy_raw[0], dy, 0, N // 2)
+        load_scales(nc.sync, 0, range(3, 4))
+        load_scales(nc.sync, 1, range(2, 4))
         load_words(2)
-        load_scales(nc.gpsimd, 1, range(4))
-        load_packed(dy_raw, dy)
-        load_scales(nc.sync, 2, range(4))
+        load_scales(nc.sync, 2, range(2))
+        load_packed(dy_raw[1], dy, N // 2, N)
         load_words(3)
         load_scales(nc.sync, 3, range(4))
         nc.sync.dma_start(out=old_sb[:], in_=old.rearrange("g (h p) n -> p (g h) n", p=P))
 
-        dst, src = views(x_raw, x_bf, 0, VECTOR_COLS)
-        nc.vector.tensor_copy(out=dst, in_=src)
-        dst, src = views(x_raw, x_bf, VECTOR_COLS, N)
+        for c0, c1 in ((0, N // 2), (N // 2, VECTOR_COLS)):
+            dst, src = views(x_raw[:, :, c0:c1], x_bf[:, c0:c1, :])
+            nc.vector.tensor_copy(out=dst, in_=src)
+        dst, src = views(x_raw[:, :, VECTOR_COLS:], x_bf[:, VECTOR_COLS:, :])
         nc.scalar.copy(out=dst, in_=src)
-        quantize(x_bf, x_codes, x_scales)
+        quantize(x_bf, x_codes, x_scales, 0, N // 2)
+        quantize(x_bf, x_codes, x_scales, N // 2, N)
         for w in range(3):
             product(w, 0)
             product(w, 1)
 
-        dst, src = views(dy_raw, dy_bf, 0, N)
-        nc.gpsimd.tensor_scalar(out=dst, in0=src, scalar1=1.0, scalar2=0.0, op0=ALU.mult, op1=ALU.add)
+        dst, src = views(dy_raw[0][:], dy_bf[:, : N // 2, :])
+        nc.vector.tensor_copy(out=dst, in_=src)
 
         copy_z1(0)
         copy_z1(1)
@@ -173,42 +182,45 @@ def tile_rows_bbilinsig_kernel(
         product(2, 3)
         sigmoid_u(0)
         sigmoid_u(1)
-        quantize(dy_bf, dy_codes, dy_scales)
-        product(3, 0)
-        product(3, 1)
         square_t(0)
         square_t(1)
         mul_ts(0)
         mul_ts(1)
         add_sq(nc.vector, 0)
-        add_sq(nc.gpsimd, 1)
+        add_sq(nc.vector, 1)
         copy_z1(2)
-        tanh_z3(2)
         copy_z1(3)
-        square_t(2)
         mul_z2(2)
-        mul_c0(0)
-        product(3, 2)
-        add_z3(2)
-        sigmoid_u(2)
-        mul_sg(0)
-        finish(nc.gpsimd, 0)
-        tanh_z3(3)
-        square_t(3)
         mul_z2(3)
-        mul_c0(1)
-        product(3, 3)
+        dst, src = views(dy_raw[1][:], dy_bf[:, N // 2 :, :])
+        nc.scalar.copy(out=dst, in_=src)
+        add_z3(2)
         add_z3(3)
+        quantize(dy_bf, dy_codes, dy_scales, 0, N)
+        product(3, 0)
+        product(3, 1)
+        tanh_z3(2)
+        sigmoid_u(2)
+        tanh_z3(3)
         sigmoid_u(3)
+        square_t(2)
+        square_t(3)
         mul_ts(2)
+        mul_c0(0)
+        mul_c0(1)
+        product(3, 2)
+        product(3, 3)
         mul_ts(3)
-        add_sq(nc.vector, 2)
+        mul_sg(0)
         mul_sg(1)
+        finish(nc.vector, 0)
+        finish(nc.vector, 1)
+        add_sq(nc.vector, 2)
         add_sq(nc.vector, 3)
-        finish(nc.gpsimd, 1)
         mul_c0(2)
         mul_c0(3)
         mul_sg(2)
         mul_sg(3)
         finish(nc.vector, 2)
-        finish(nc.vector, 3)
+        finish(nc.vector, 3, 0, N // 2)
+        finish(nc.vector, 3, N // 2, N)

@@ -44,15 +44,15 @@ def tile_rows_bbilinsig_kernel(
         x_scales = sb.tile([P, N], U8, name="x_scales", align_bytes=64)
         dy_scales = sb.tile([P, N], U8, name="dy_scales", align_bytes=64)
         zero = sb.tile([P, 1], F32, name="zero")
-        half = sb.tile([P, 1], F32, name="half")
+        warm = sb.tile([P, 1], F32, name="warm")
         bank = [[ps.tile([P, N], F32, name="bank%d_%d" % (w, g)) for g in range(G)] for w in range(4)]
 
-        def stage(name):
-            return [sb.tile([P, N], F32, name="%s%d" % (name, i)) for i in range(4)]
-
-        z1c, prod, u, th, sg, sq, ts, n_, gc, neg, res = [
-            stage(nm) for nm in ("z1c", "prod", "u", "th", "sg", "sq", "ts", "n", "gc", "neg", "res")
+        z1c, prod, u, th, sg, wv, q0, gc, neg, res = [
+            sb.tile([P, 4 * N], F32, name=nm) for nm in ("z1c", "prod", "u", "th", "sg", "wv", "q0", "gc", "neg", "res")
         ]
+
+        def cols(i, count=1):
+            return slice(N * i, N * (i + count))
 
         def load_words(w):
             nc.sync.dma_start(
@@ -94,47 +94,46 @@ def tile_rows_bbilinsig_kernel(
             )
 
         def copy_z1(i):
-            nc.scalar.copy(out=z1c[i][:], in_=bank[0][i % G][:])
+            nc.scalar.copy(out=z1c[:, cols(i)], in_=bank[0][i % G][:])
 
         def mul_z2(i):
-            nc.vector.tensor_tensor(out=prod[i][:], in0=z1c[i][:], in1=bank[1][i % G][:], op=ALU.mult)
+            nc.vector.tensor_tensor(out=prod[:, cols(i)], in0=z1c[:, cols(i)], in1=bank[1][i % G][:], op=ALU.mult)
 
         def add_z3(i):
-            nc.vector.tensor_tensor(out=u[i][:], in0=prod[i][:], in1=bank[2][i % G][:], op=ALU.add)
+            nc.vector.tensor_tensor(out=u[:, cols(i)], in0=prod[:, cols(i)], in1=bank[2][i % G][:], op=ALU.add)
 
         def tanh_z3(i):
-            nc.scalar.activation(out=th[i][:], in_=bank[2][i % G][:], func=ACT.Tanh)
+            nc.scalar.activation(out=th[:, cols(i)], in_=bank[2][i % G][:], func=ACT.Tanh)
 
         def sigmoid_u(i):
-            nc.scalar.activation(out=sg[i][:], in_=u[i][:], func=ACT.Sigmoid)
+            nc.scalar.activation(out=sg[:, cols(i)], in_=u[:, cols(i)], func=ACT.Sigmoid)
 
-        def square_t(i):
-            nc.scalar.activation(out=sq[i][:], in_=th[i][:], func=ACT.Square, bias=half[:], scale=-1.0)
+        def add_th(i):
+            nc.vector.scalar_tensor_tensor(
+                out=wv[:, cols(i)], in0=sg[:, cols(i)], scalar=1.0, in1=th[:, cols(i)], op0=ALU.subtract, op1=ALU.add
+            )
 
-        def mul_ts(i):
-            nc.vector.tensor_tensor(out=ts[i][:], in0=th[i][:], in1=sg[i][:], op=ALU.mult)
-
-        def add_sq(engine, i):
-            engine.tensor_tensor(out=n_[i][:], in0=ts[i][:], in1=sq[i][:], op=ALU.add)
+        def mul_th(engine, i, count=1):
+            c = cols(i, count)
+            engine.tensor_tensor(out=q0[:, c], in0=wv[:, c], in1=th[:, c], op=ALU.mult)
 
         def mul_c0(i):
             nc.vector.scalar_tensor_tensor(
-                out=gc[i][:], in0=n_[i][:], scalar=1.25, in1=bank[3][i % G][:], op0=ALU.subtract, op1=ALU.mult
+                out=gc[:, cols(i)], in0=q0[:, cols(i)], scalar=1.0, in1=bank[3][i % G][:], op0=ALU.subtract, op1=ALU.mult
             )
 
         def mul_sg(i):
-            nc.vector.tensor_tensor(out=neg[i][:], in0=gc[i][:], in1=sg[i][:], op=ALU.mult)
+            nc.vector.tensor_tensor(out=neg[:, cols(i)], in0=gc[:, cols(i)], in1=sg[:, cols(i)], op=ALU.mult)
 
         def finish(engine, i, c0=0, c1=N):
             h, g = divmod(i, G)
-            engine.tensor_tensor(
-                out=res[i][:, c0:c1], in0=old_sb[:, 2 * g + h, c0:c1], in1=neg[i][:, c0:c1], op=ALU.subtract
-            )
-            nc.sync.dma_start(out=out[g, P * h : P * (h + 1), c0:c1], in_=res[i][:, c0:c1])
+            c = slice(N * i + c0, N * i + c1)
+            engine.tensor_tensor(out=res[:, c], in0=old_sb[:, 2 * g + h, c0:c1], in1=neg[:, c], op=ALU.subtract)
+            nc.sync.dma_start(out=out[g, P * h : P * (h + 1), c0:c1], in_=res[:, c])
 
         nc.vector.memset(plane[:].bitcast(I32), 0)
-        nc.gpsimd.memset(zero[:], 0.0)
-        nc.scalar.activation(out=half[:], in_=zero[:], func=ACT.Sigmoid)
+        nc.vector.memset(zero[:], 0.0)
+        nc.scalar.activation(out=warm[:], in_=zero[:], func=ACT.Sigmoid)
 
         load_words(0)
         load_packed(x_raw, x, 0, N)
@@ -142,12 +141,12 @@ def tile_rows_bbilinsig_kernel(
         load_scales(nc.sync, 0, range(2))
         load_scales(nc.sync, 1, range(2))
         load_scales(nc.sync, 0, range(2, 3))
-        load_scales(nc.gpsimd, 2, range(2, 4))
+        load_scales(nc.gpsimd, 0, range(3, 4))
+        load_scales(nc.gpsimd, 1, range(2, 4))
+        load_scales(nc.gpsimd, 2, range(3, 4))
         load_packed(dy_raw[0], dy, 0, N // 2)
-        load_scales(nc.sync, 0, range(3, 4))
-        load_scales(nc.sync, 1, range(2, 4))
         load_words(2)
-        load_scales(nc.sync, 2, range(2))
+        load_scales(nc.sync, 2, range(3))
         load_packed(dy_raw[1], dy, N // 2, N)
         load_words(3)
         load_scales(nc.sync, 3, range(4))
@@ -166,6 +165,14 @@ def tile_rows_bbilinsig_kernel(
 
         dst, src = views(dy_raw[0][:], dy_bf[:, : N // 2, :])
         nc.vector.tensor_copy(out=dst, in_=src)
+        nc.gpsimd.tensor_scalar(
+            out=dy_bf[:, N // 2 :, :],
+            in0=dy_raw[1][:].rearrange("p j n -> p n j"),
+            scalar1=1.0,
+            scalar2=0.0,
+            op0=ALU.mult,
+            op1=ALU.add,
+        )
 
         copy_z1(0)
         copy_z1(1)
@@ -182,41 +189,34 @@ def tile_rows_bbilinsig_kernel(
         product(2, 3)
         sigmoid_u(0)
         sigmoid_u(1)
-        square_t(0)
-        square_t(1)
-        mul_ts(0)
-        mul_ts(1)
-        add_sq(nc.vector, 0)
-        add_sq(nc.vector, 1)
+        quantize(dy_bf, dy_codes, dy_scales, 0, N)
+        product(3, 0)
+        product(3, 1)
+        add_th(0)
+        add_th(1)
+        mul_th(nc.gpsimd, 0, 2)
         copy_z1(2)
         copy_z1(3)
         mul_z2(2)
         mul_z2(3)
-        dst, src = views(dy_raw[1][:], dy_bf[:, N // 2 :, :])
-        nc.scalar.copy(out=dst, in_=src)
+        tanh_z3(2)
+        tanh_z3(3)
         add_z3(2)
         add_z3(3)
-        quantize(dy_bf, dy_codes, dy_scales, 0, N)
-        product(3, 0)
-        product(3, 1)
-        tanh_z3(2)
         sigmoid_u(2)
-        tanh_z3(3)
         sigmoid_u(3)
-        square_t(2)
-        square_t(3)
-        mul_ts(2)
+        add_th(2)
+        add_th(3)
+        mul_th(nc.gpsimd, 3)
         mul_c0(0)
         mul_c0(1)
         product(3, 2)
         product(3, 3)
-        mul_ts(3)
         mul_sg(0)
-        mul_sg(1)
+        mul_th(nc.vector, 2)
         finish(nc.vector, 0)
-        finish(nc.vector, 1)
-        add_sq(nc.vector, 2)
-        add_sq(nc.vector, 3)
+        mul_sg(1)
+        finish(nc.gpsimd, 1)
         mul_c0(2)
         mul_c0(3)
         mul_sg(2)

@@ -122,8 +122,9 @@ def tile_rows_bbilinsig_kernel(
                 out=gc[:, cols(i)], in0=q0[:, cols(i)], scalar=1.0, in1=bank[3][i % G][:], op0=ALU.subtract, op1=ALU.mult
             )
 
-        def mul_sg(i):
-            nc.vector.tensor_tensor(out=neg[:, cols(i)], in0=gc[:, cols(i)], in1=sg[:, cols(i)], op=ALU.mult)
+        def mul_sg(i, c0=0, c1=N):
+            c = slice(N * i + c0, N * i + c1)
+            nc.vector.tensor_tensor(out=neg[:, c], in0=gc[:, c], in1=sg[:, c], op=ALU.mult)
 
         def finish(engine, i, c0=0, c1=N):
             h, g = divmod(i, G)
@@ -142,11 +143,11 @@ def tile_rows_bbilinsig_kernel(
         load_scales(nc.sync, 1, range(2))
         load_scales(nc.sync, 0, range(2, 3))
         load_scales(nc.gpsimd, 0, range(3, 4))
-        load_scales(nc.gpsimd, 1, range(2, 4))
-        load_scales(nc.gpsimd, 2, range(3, 4))
+        load_scales(nc.gpsimd, 1, range(2, 3))
         load_packed(dy_raw[0], dy, 0, N // 2)
+        load_scales(nc.sync, 1, range(3, 4))
         load_words(2)
-        load_scales(nc.sync, 2, range(3))
+        load_scales(nc.sync, 2, range(4))
         load_packed(dy_raw[1], dy, N // 2, N)
         load_words(3)
         load_scales(nc.sync, 3, range(4))
@@ -165,6 +166,7 @@ def tile_rows_bbilinsig_kernel(
 
         dst, src = views(dy_raw[0][:], dy_bf[:, : N // 2, :])
         nc.vector.tensor_copy(out=dst, in_=src)
+        quantize(dy_bf, dy_codes, dy_scales, 0, N // 2)
         nc.gpsimd.tensor_scalar(
             out=dy_bf[:, N // 2 :, :],
             in0=dy_raw[1][:].rearrange("p j n -> p n j"),
@@ -189,12 +191,13 @@ def tile_rows_bbilinsig_kernel(
         product(2, 3)
         sigmoid_u(0)
         sigmoid_u(1)
-        quantize(dy_bf, dy_codes, dy_scales, 0, N)
+        quantize(dy_bf, dy_codes, dy_scales, N // 2, N)
         product(3, 0)
         product(3, 1)
         add_th(0)
         add_th(1)
-        mul_th(nc.gpsimd, 0, 2)
+        mul_th(nc.gpsimd, 0)
+        mul_th(nc.gpsimd, 1)
         copy_z1(2)
         copy_z1(3)
         mul_z2(2)
@@ -207,20 +210,21 @@ def tile_rows_bbilinsig_kernel(
         sigmoid_u(3)
         add_th(2)
         add_th(3)
-        mul_th(nc.gpsimd, 3)
+        mul_th(nc.gpsimd, 2)
         mul_c0(0)
         mul_c0(1)
         product(3, 2)
         product(3, 3)
         mul_sg(0)
-        mul_th(nc.vector, 2)
-        finish(nc.vector, 0)
+        mul_th(nc.vector, 3)
         mul_sg(1)
+        finish(nc.vector, 0)
         finish(nc.gpsimd, 1)
         mul_c0(2)
         mul_c0(3)
         mul_sg(2)
-        mul_sg(3)
+        mul_sg(3, 0, N // 2)
         finish(nc.vector, 2)
+        mul_sg(3, N // 2, N)
         finish(nc.vector, 3, 0, N // 2)
         finish(nc.vector, 3, N // 2, N)

from contextlib import ExitStack

import concourse.mybir as mybir

G, D, M, N = 2, 256, 256, 512
FLOPS = 2 * 4 * G * D * M * N

F32 = mybir.dt.float32
BF16 = mybir.dt.bfloat16
I32 = mybir.dt.int32
U32 = mybir.dt.uint32
U8 = mybir.dt.uint8
FP8X4 = mybir.dt.float8_e4m3fn_x4
FP4X4 = mybir.dt.float4_e2m1fn_x4
ACT = mybir.ActivationFunctionType
ALU = mybir.AluOpType

P = 128
PACK = 4
ROWS = 64
VECTOR_COLS = 320


def tile_rows_bbilinsig_kernel(
    tc, x, w1_words, w1_scales, w2_words, w2_scales, w3_words, w3_scales, wo_words, wo_scales, dy, old, out
):
    nc = tc.nc
    with ExitStack() as ctx:
        sb = ctx.enter_context(tc.tile_pool(name="sb", bufs=1))
        ps = ctx.enter_context(tc.psum_pool(name="ps", bufs=1))
        ctx.enter_context(tc.manual_schedule())

        w_dram = [w1_words, w2_words, w3_words, wo_words]
        s_dram = [w1_scales, w2_scales, w3_scales, wo_scales]
        words = [sb.tile([P, 2 * M], U8, name="words%d" % w, align_bytes=64) for w in range(4)]
        plane = sb.tile([P, 4 * M], U8, name="plane", align_bytes=64)
        x_raw = sb.tile([P, PACK, N], F32, name="x_raw")
        dy_raw = [sb.tile([P, PACK, N // 2], F32, name="dy_raw%d" % k) for k in range(2)]
        old_sb = sb.tile([P, 4, N], F32, name="old_sb")
        x_bf = sb.tile([P, N, PACK], BF16, name="x_bf", align_bytes=64)
        dy_bf = sb.tile([P, N, PACK], BF16, name="dy_bf", align_bytes=64)
        x_codes = sb.tile([P, N], U32, name="x_codes", align_bytes=64)
        dy_codes = sb.tile([P, N], U32, name="dy_codes", align_bytes=64)
        x_scales = sb.tile([P, N], U8, name="x_scales", align_bytes=64)
        dy_scales = sb.tile([P, N], U8, name="dy_scales", align_bytes=64)
        zero = sb.tile([P, 1], F32, name="zero")
        warm = sb.tile([P, 1], F32, name="warm")
        bank = [[ps.tile([P, N], F32, name="bank%d_%d" % (w, g)) for g in range(G)] for w in range(4)]

        z1c, prod, u, th, sg, wv, q0, gc, neg, res = [
            sb.tile([P, 4 * N], F32, name=nm) for nm in ("z1c", "prod", "u", "th", "sg", "wv", "q0", "gc", "neg", "res")
        ]

        def cols(i, count=1):
            return slice(N * i, N * (i + count))

        def load_words(w):
            nc.sync.dma_start(
                out=words[w][:].bitcast(I32), in_=w_dram[w].rearrange("g p b -> (g p) b").bitcast(I32)
            )

        def load_scales(engine, w, quads):
            rows = s_dram[w].rearrange("g (c r) m -> (g c) r m", r=4)
            for q in quads:
                engine.dma_start(
                    out=plane[32 * q : 32 * q + 4, M * w : M * (w + 1)].bitcast(I32), in_=rows[q].bitcast(I32)
                )

        def load_packed(raw, src, c0, c1):
            nc.sync.dma_start(out=raw[:], in_=src.rearrange("g (p j) n -> (g p) j n", j=PACK)[:, :, c0:c1])

        def views(raw, bf):
            return bf.rearrange("p (c i) j -> p c j i", i=4), raw.rearrange("p j (c i) -> p c j i", i=4)

        def quantize(bf, codes, scales, c0, c1):
            nc.vector.quantize_mx(
                out=codes[:, c0:c1].bitcast(FP8X4),
                scales=scales[:, c0:c1],
                in_=bf[:, c0:c1, :].rearrange("p n j -> p (n j)"),
            )

        def product(w, i):
            h, g = divmod(i, G)
            rows = slice(ROWS * g, ROWS * (g + 1))
            codes, scales = (dy_codes, dy_scales) if w == 3 else (x_codes, x_scales)
            nc.tensor.matmul_mx(
                out=bank[w][g][:],
                lhsT=words[w][rows, 2 * P * h : 2 * P * (h + 1)].bitcast(FP4X4),
                lhsT_scale=plane[rows, M * w + P * h : M * w + P * (h + 1)],
                rhs=codes[rows, :].bitcast(FP8X4),
                rhs_scale=scales[rows, :],
                start=True,
                stop=True,
            )

        def copy_z1(i):
            nc.scalar.copy(out=z1c[:, cols(i)], in_=bank[0][i % G][:])

        def mul_z2(i):
            nc.vector.tensor_tensor(out=prod[:, cols(i)], in0=z1c[:, cols(i)], in1=bank[1][i % G][:], op=ALU.mult)

        def add_z3(i):
            nc.vector.tensor_tensor(out=u[:, cols(i)], in0=prod[:, cols(i)], in1=bank[2][i % G][:], op=ALU.add)

        def tanh_z3(i):
            nc.scalar.activation(out=th[:, cols(i)], in_=bank[2][i % G][:], func=ACT.Tanh)

        def sigmoid_u(i):
            nc.scalar.activation(out=sg[:, cols(i)], in_=u[:, cols(i)], func=ACT.Sigmoid)

        def add_th(i):
            nc.vector.scalar_tensor_tensor(
                out=wv[:, cols(i)], in0=sg[:, cols(i)], scalar=1.0, in1=th[:, cols(i)], op0=ALU.subtract, op1=ALU.add
            )

        def mul_th(engine, i, count=1):
            c = cols(i, count)
            engine.tensor_tensor(out=q0[:, c], in0=wv[:, c], in1=th[:, c], op=ALU.mult)

        def mul_c0(i):
            nc.vector.scalar_tensor_tensor(
                out=gc[:, cols(i)], in0=q0[:, cols(i)], scalar=1.0, in1=bank[3][i % G][:], op0=ALU.subtract, op1=ALU.mult
            )

        def mul_sg(i, c0=0, c1=N):
            c = slice(N * i + c0, N * i + c1)
            nc.vector.tensor_tensor(out=neg[:, c], in0=gc[:, c], in1=sg[:, c], op=ALU.mult)

        def finish(engine, i, c0=0, c1=N):
            h, g = divmod(i, G)
            c = slice(N * i + c0, N * i + c1)
            engine.tensor_tensor(out=res[:, c], in0=old_sb[:, 2 * g + h, c0:c1], in1=neg[:, c], op=ALU.subtract)
            nc.sync.dma_start(out=out[g, P * h : P * (h + 1), c0:c1], in_=res[:, c])

        nc.vector.memset(plane[:].bitcast(I32), 0)
        nc.vector.memset(zero[:], 0.0)
        nc.scalar.activation(out=warm[:], in_=zero[:], func=ACT.Sigmoid)

        load_words(0)
        load_packed(x_raw, x, 0, N)
        load_words(1)
        load_scales(nc.sync, 0, range(2))
        load_scales(nc.sync, 1, range(2))
        load_scales(nc.sync, 0, range(2, 3))
        load_scales(nc.gpsimd, 0, range(3, 4))
        load_scales(nc.gpsimd, 1, range(2, 3))
        load_packed(dy_raw[0], dy, 0, N // 2)
        load_scales(nc.sync, 1, range(3, 4))
        load_words(2)
        load_scales(nc.sync, 2, range(4))
        load_packed(dy_raw[1], dy, N // 2, N)
        load_words(3)
        load_scales(nc.sync, 3, range(4))
        nc.sync.dma_start(out=old_sb[:], in_=old.rearrange("g (h p) n -> p (g h) n", p=P))

        for c0, c1 in ((0, N // 2), (N // 2, VECTOR_COLS)):
            dst, src = views(x_raw[:, :, c0:c1], x_bf[:, c0:c1, :])
            nc.vector.tensor_copy(out=dst, in_=src)
        dst, src = views(x_raw[:, :, VECTOR_COLS:], x_bf[:, VECTOR_COLS:, :])
        nc.scalar.copy(out=dst, in_=src)
        quantize(x_bf, x_codes, x_scales, 0, N // 2)
        quantize(x_bf, x_codes, x_scales, N // 2, N)
        for w in range(3):
            product(w, 0)
            product(w, 1)

        dst, src = views(dy_raw[0][:], dy_bf[:, : N // 2, :])
        nc.vector.tensor_copy(out=dst, in_=src)
        quantize(dy_bf, dy_codes, dy_scales, 0, N // 2)
        nc.gpsimd.tensor_scalar(
            out=dy_bf[:, N // 2 :, :],
            in0=dy_raw[1][:].rearrange("p j n -> p n j"),
            scalar1=1.0,
            scalar2=0.0,
            op0=ALU.mult,
            op1=ALU.add,
        )

        copy_z1(0)
        copy_z1(1)
        mul_z2(0)
        mul_z2(1)
        for w in range(2):
            product(w, 2)
            product(w, 3)
        tanh_z3(0)
        tanh_z3(1)
        add_z3(0)
        add_z3(1)
        product(2, 2)
        product(2, 3)
        sigmoid_u(0)
        sigmoid_u(1)
        quantize(dy_bf, dy_codes, dy_scales, N // 2, N)
        product(3, 0)
        product(3, 1)
        add_th(0)
        add_th(1)
        mul_th(nc.gpsimd, 0)
        mul_th(nc.gpsimd, 1)
        copy_z1(2)
        copy_z1(3)
        mul_z2(2)
        mul_z2(3)
        tanh_z3(2)
        tanh_z3(3)
        add_z3(2)
        add_z3(3)
        sigmoid_u(2)
        sigmoid_u(3)
        add_th(2)
        add_th(3)
        mul_th(nc.gpsimd, 2)
        mul_c0(0)
        mul_c0(1)
        product(3, 2)
        product(3, 3)
        mul_sg(0)
        mul_th(nc.vector, 3)
        mul_sg(1)
        finish(nc.vector, 0)
        finish(nc.gpsimd, 1)
        mul_c0(2)
        mul_c0(3)
        mul_sg(2)
        mul_sg(3, 0, N // 2)
        finish(nc.vector, 2)
        mul_sg(3, N // 2, N)
        finish(nc.vector, 3, 0, N // 2)
        finish(nc.vector, 3, N // 2, N)
